import numpy as np
import ml_dtypes


def mxq(x, axis, fmt="e4m3"):
    dtype, down = {"e4m3": (ml_dtypes.float8_e4m3fn, 7), "e5m2": (ml_dtypes.float8_e5m2, 14)}[fmt]
    v = np.moveaxis(np.asarray(x, np.float32).astype(ml_dtypes.bfloat16).astype(np.float64), axis, -1)
    blocks = v.reshape(v.shape[:-1] + (-1, 32))
    amax = np.abs(blocks).max(-1, keepdims=True)
    byte = np.maximum(np.where(amax > 0, np.frexp(amax)[1] - 1 + 127, 0) - down, 1)
    scale = np.exp2(byte - 127.0)
    codes = (blocks / scale).astype(np.float32).astype(dtype).astype(np.float64)
    return np.moveaxis((codes * scale).reshape(v.shape), -1, axis)


WIDE = False


def mx_kscale(k):
    if not WIDE:
        return np.ones(k)
    levels = np.array([10, -10, 5, -5, 0])
    if k % 512:
        return np.exp2(np.random.permutation(np.resize(levels, k // 32))).repeat(32)
    a = np.empty((k // 512, 16))
    for p in range(k // 512):
        a[p, :8] = np.random.permutation(np.resize(levels, 8))
        for g in range(8):
            far = levels[np.abs(levels - a[p, g]) >= 10]
            a[p, g + 8] = far[np.random.randint(len(far))]
    return np.exp2(a.ravel()).repeat(32)


def f64(x):
    return np.asarray(x).astype(np.float64)


def striped(idx):
    return np.tile(idx.reshape(-1, 16).T, (8, 1)).astype(np.uint16)


def unstriped(offs):
    return offs[:16].T.reshape(-1).astype(np.int64)


def striped8(idx):
    return np.concatenate([x.reshape(-1, 16).T for x in idx]).astype(np.uint16)


def runs(offs, k):
    lists = np.stack([offs[16 * r : 16 * r + 16].T.reshape(-1) for r in range(8)]).astype(np.int64)
    return lists[np.arange(k) % 512 // 64]


def pack_weight(w):
    k, n = w.shape
    w = f64(np.asarray(w, np.float32).astype(ml_dtypes.bfloat16)).reshape(k // 32, 32, n)
    amax = np.abs(w).max(1)
    byte = np.clip(np.where(amax > 0, np.frexp(amax)[1] - 1 + 127 - 7, 1), 1, 254)
    scaled = (w * np.exp2(127.0 - byte)[:, None, :]).reshape(k, n).astype(np.float32)
    words = np.ascontiguousarray(scaled.reshape(k // 512, 128, 4, n).transpose(0, 1, 3, 2)).astype(ml_dtypes.float8_e4m3fn).view(np.uint8)
    return words, np.ascontiguousarray(byte.astype(np.uint8).reshape(k // 512, 16, n))


def unpack_weight(words, scales):
    g, p, n, _ = words.shape
    vals = np.ascontiguousarray(words).view(ml_dtypes.float8_e4m3fn).astype(np.float64) * np.repeat(np.exp2(scales.astype(np.float64) - 127.0), 8, axis=1)[..., None]
    return vals.transpose(0, 1, 3, 2).reshape(g * 512, n)


def silu(v):
    return v / (1.0 + np.exp(-np.maximum(v, -700.0)))

def planes(y):
    n, m = y.shape
    v = y.astype(np.float32).astype(ml_dtypes.bfloat16).astype(np.float64).reshape(n // 32, 32, m)
    top = np.abs(v).max(1)
    byte = np.clip(np.where(top > 0, np.frexp(top)[1] - 1 + 127 - 7, 1), 1, 254)
    codes = (v * np.exp2(127.0 - byte)[:, None, :]).reshape(n, m).astype(np.float32).astype(ml_dtypes.float8_e4m3fn).view(np.uint8)
    words = codes.reshape(n // 512, 128, 4, m).transpose(0, 1, 3, 2)
    return np.ascontiguousarray(words), np.ascontiguousarray(byte.astype(np.uint8).reshape(n // 512, 16, m))


K, T, S, G, H = 512, 2048, 512, 2048, 512


def setup_inputs():
    n = np.random.standard_normal
    s = mx_kscale(K)[:, None]
    packed_xT = pack_weight(n((K, T)) * s)
    packed_dT = pack_weight(n((K, G)) / s)
    return {
        "x_words": packed_xT[0],
        "x_scales": packed_xT[1],
        "d_words": packed_dT[0],
        "d_scales": packed_dT[1],
        "gs": (np.random.uniform(0.5, 1.5, (K, 1)) * s).astype(np.float32),
        "offs": striped(np.random.permutation(T)[:S]),
        "k1": striped8(np.random.randint(0, G, (8, H))),
        "nb": striped8(np.stack([np.random.permutation(S) for _ in range(8)])),
        "k2": striped8(np.random.randint(0, G, (8, H))),
    }


def reference(x_words, x_scales, d_words, d_scales, gs, offs, k1, nb, k2):
    d_k2 = unpack_weight(d_words, d_scales)[np.arange(K)[:, None], runs(k2, K)]
    d_k1 = unpack_weight(d_words, d_scales)[np.arange(K)[:, None], runs(k1, K)]
    xq = unpack_weight(x_words, x_scales)[:, unstriped(offs)]
    h = 0.0625 * (d_k1.T @ xq)
    z = f64(gs) * (silu(h - (h[np.arange(H)[:, None], runs(nb, H)])))
    out_0 = 0.0625 * ((d_k2.T @ mxq(z, 0, "e4m3")))
    return (out_0,) + planes(out_0)

from contextlib import ExitStack

import concourse.mybir as mybir

F32 = mybir.dt.float32
BF16 = mybir.dt.bfloat16
I32 = mybir.dt.int32
U32 = mybir.dt.uint32
U16 = mybir.dt.uint16
U8 = mybir.dt.uint8
FP8X4 = mybir.dt.float8_e4m3fn_x4
ACT = mybir.ActivationFunctionType
ALU = mybir.AluOpType

P = 128
PACK = 4
TABLE = 2048
N = 512
HALF = N // 2
SIXTEENTH = 0.0625
CHUNK = 128
FLOPS = 2 * 2 * 512 * 512 * 512


def tile_picked_pqnbr_silu_po_kernel(
    tc, x_words, x_scales, d_words, d_scales, gs, offs, k1, nb, k2, out_0, out_1, out_2
):
    nc = tc.nc
    with ExitStack() as ctx:
        keep = ctx.enter_context(tc.tile_pool(name="keep", bufs=1))
        shared = ctx.enter_context(tc.tile_pool(name="shared", bufs=1))
        psum = ctx.enter_context(tc.psum_pool(name="psum", bufs=1))

        def load_list(name, src):
            t = keep.tile([P, N // 16], U16, name=name)
            nc.sync.dma_start(t[:], src)
            return t

        def deal(dst, src):
            nc.vector.tensor_copy(
                dst.rearrange("p (t m) -> p m t", t=PACK), src.rearrange("p (m t) -> p m t", t=PACK)
            )

        def place(queue, dst, src):
            for i in range(PACK):
                queue.dma_start(dst[i:P:32, :].bitcast(I32), src[8 * i : P : 32, :].bitcast(I32))

        d_rows = keep.tile([P, TABLE], U8, name="d_rows", align_bytes=64)
        x_rows = keep.tile([P, TABLE], U8, name="x_rows", align_bytes=64)
        d_table = keep.tile([P, TABLE], I32, name="d_table", align_bytes=64)
        x_table = shared.tile([P, TABLE], I32, name="x_table", align_bytes=64, offset=0)
        placed1 = keep.tile([P, 2 * N], U8, name="placed1", align_bytes=64)
        placed2 = keep.tile([P, N], U8, name="placed2", align_bytes=64)
        warm = keep.tile([P, 8], F32, name="warm")
        warm_out = keep.tile([P, 8], F32, name="warm_out")
        nc.vector.memset(d_rows[:].bitcast(I32), 0)
        nc.vector.memset(x_rows[:].bitcast(I32), 0)
        nc.vector.memset(d_table[:, 0:8], 0)
        nc.vector.memset(x_table[:, 0:8], 0)
        nc.vector.memset(warm[:], 0.0)
        nc.vector.memset(placed1[:].bitcast(I32), 0)
        nc.vector.memset(placed2[:].bitcast(I32), 0)
        nc.scalar.dma_start(d_rows[0:P:8, :].bitcast(I32), d_scales[0].bitcast(I32))
        nc.scalar.dma_start(x_rows[0:P:8, :].bitcast(I32), x_scales[0].bitcast(I32))
        nc.scalar.activation(warm_out[:], warm[:], ACT.Silu)

        k1_list = load_list("k1_list", k1)
        offs_list = load_list("offs_list", offs)
        k2_list = load_list("k2_list", k2)
        nb_list = load_list("nb_list", nb)
        gain = keep.tile([P, PACK], F32, name="gain")
        nc.sync.dma_start(gain[:], gs.rearrange("(p t) o -> p (t o)", t=PACK))
        nc.sync.dma_start(d_table[:], d_words[0].rearrange("p c r -> p (c r)").bitcast(I32))
        nc.sync.dma_start(x_table[:], x_words[0].rearrange("p c r -> p (c r)").bitcast(I32))

        w1_rows = keep.tile([P, N], U8, name="w1_rows", align_bytes=64)
        xp_rows = keep.tile([P, N], U8, name="xp_rows", align_bytes=64)
        staged1 = keep.tile([P, 2 * N], U8, name="staged1", align_bytes=64)
        nc.vector.tensor_copy(w1_rows[:], d_rows[:].indirect(k1_list[:]))
        nc.vector.tensor_copy(xp_rows[:], x_rows[:].indirect(offs_list[:]))
        deal(staged1[:, 0:N], w1_rows[:])
        nc.vector.tensor_copy(staged1[:, N : 2 * N].bitcast(I32), xp_rows[:].bitcast(I32))
        place(nc.scalar, placed1, staged1)

        w1_picked = keep.tile([P, N], U32, name="w1_picked", align_bytes=64)
        nc.vector.tensor_copy(w1_picked[:], d_table[:].bitcast(U32).indirect(k1_list[:]))
        w1_words = keep.tile([P, N], U32, name="w1_words", align_bytes=64)
        deal(w1_words[:], w1_picked[:])
        x_picked = []
        for a in range(2):
            half = keep.tile([P, HALF], U32, name="x_picked%d" % a, align_bytes=64)
            entries = offs_list[:, a * HALF // 16 : (a + 1) * HALF // 16]
            nc.vector.tensor_copy(half[:], x_table[:].bitcast(U32).indirect(entries))
            x_picked.append(half)

        h_banks = {}
        for pair in range(2):
            for a in range(2):
                for t in (2 * pair, 2 * pair + 1):
                    bank = psum.tile([P, HALF], F32, name="h_bank", tag="bank%d" % (2 * t + a))
                    cols = slice(P * t, P * (t + 1))
                    nc.tensor.matmul_mx(
                        out=bank[:],
                        lhsT=w1_words[:, cols].bitcast(FP8X4),
                        lhsT_scale=placed1[:, cols],
                        rhs=x_picked[a][:].bitcast(FP8X4),
                        rhs_scale=placed1[:, N + a * HALF : N + (a + 1) * HALF],
                        start=True,
                        stop=True,
                    )
                    h_banks[t, a] = bank

        w2_rows = shared.tile([P, N], U8, name="w2_rows", align_bytes=64, offset=0)
        staged2 = keep.tile([P, N], U8, name="staged2", align_bytes=64)
        nc.vector.tensor_copy(w2_rows[:], d_rows[:].indirect(k2_list[:]))
        w2_picked = shared.tile([P, N], U32, name="w2_picked", align_bytes=64, offset=2048)
        deal(staged2[:], w2_rows[:])
        place(nc.sync, placed2, staged2)
        nc.vector.tensor_copy(w2_picked[:], d_table[:].bitcast(U32).indirect(k2_list[:]))
        w2_words = keep.tile([P, N], U32, name="w2_words", align_bytes=64)
        deal(w2_words[:], w2_picked[:])

        windows = []
        own = {}
        for t in range(PACK):
            window = keep.tile([P, N], F32, name="window%d" % t)
            own[t, 0] = keep.tile([P, HALF], F32, name="own%d_0" % t)
            own[t, 1] = keep.tile([P, HALF], F32, name="own%d_1" % t, tag="late%d" % t, align_bytes=64)
            nc.scalar.copy(window[:, 0:HALF], h_banks[t, 0][:])
            nc.scalar.copy(own[t, 0][:], h_banks[t, 0][:])
            nc.scalar.copy(window[:, HALF:N], h_banks[t, 1][:])
            nc.sync.dma_start(own[t, 1][:], window[:, HALF:N])
            windows.append(window)

        out_codes = keep.tile([P, N], U32, name="out_codes", align_bytes=64)
        out_scales = keep.tile([P, N], U8, name="out_scales", align_bytes=64)
        out_rows = out_0.rearrange("(p t) j -> p t j", t=PACK)
        out_words = out_1[0].rearrange("p c r -> p (c r)").bitcast(I32)

        chunks = range(N // CHUNK)
        z_parts = []
        for c in chunks:
            j0 = c * CHUNK
            diff = keep.tile([P, PACK, CHUNK], F32, name="diff%d" % c)
            act = keep.tile([P, PACK, CHUNK], F32, name="act%d" % c)
            z_planes = keep.tile([P, PACK, CHUNK], BF16, name="z_planes%d" % c)
            for t in range(PACK):
                nc.vector.tensor_tensor(
                    diff[:, t, :],
                    windows[t][:].indirect(nb_list[:, j0 // 16 : (j0 + CHUNK) // 16]),
                    own[t, j0 // HALF][:, j0 % HALF : j0 % HALF + CHUNK],
                    ALU.subtract,
                )
            for t in range(PACK):
                nc.scalar.activation(act[:, t, :], diff[:, t, :], ACT.Silu, scale=-SIXTEENTH)
            for t in range(PACK):
                nc.scalar.activation(
                    z_planes[:, t, :], act[:, t, :], ACT.Copy, scale=gain[:, t : t + 1]
                )
            z_parts.append(z_planes)

        y_banks = []
        for c in chunks:
            z_woven = keep.tile([P, CHUNK, PACK], BF16, name="z_woven%d" % c, tag="late%d" % (3 - c), align_bytes=64)
            nc.vector.tensor_copy(
                z_woven[:].rearrange("p (c i) t -> p c t i", i=4),
                z_parts[c][:].rearrange("p t (c i) -> p c t i", i=4),
            )
            z_codes = keep.tile([P, CHUNK], U32, name="z_codes%d" % c, align_bytes=64)
            z_scales = keep.tile([P, CHUNK], U8, name="z_scales%d" % c, align_bytes=64)
            nc.vector.quantize_mx(
                out=z_codes[:].bitcast(FP8X4),
                scales=z_scales[:],
                in_=z_woven[:].rearrange("p j t -> p (j t)"),
            )
            bank = psum.tile([P, PACK, CHUNK], F32, name="y_bank", tag="bank%d" % c)
            for t in range(PACK):
                cols = slice(P * t, P * (t + 1))
                nc.tensor.matmul_mx(
                    out=bank[:, t, :],
                    lhsT=w2_words[:, cols].bitcast(FP8X4),
                    lhsT_scale=placed2[:, cols],
                    rhs=z_codes[:].bitcast(FP8X4),
                    rhs_scale=z_scales[:],
                    start=True,
                    stop=True,
                )
            y_banks.append(bank)

        for c in chunks:
            cols_j = slice(c * CHUNK, (c + 1) * CHUNK)
            y = keep.tile([P, PACK, CHUNK], F32, name="y%d" % c)
            nc.scalar.activation(y[:], y_banks[c][:], ACT.Copy, scale=SIXTEENTH)
            nc.sync.dma_start(out_rows[:, :, cols_j], y[:])
            y_woven = keep.tile([P, CHUNK, PACK], BF16, name="y_woven%d" % c, align_bytes=64)
            nc.vector.tensor_copy(
                y_woven[:].rearrange("p (c i) t -> p c t i", i=4),
                y[:].rearrange("p t (c i) -> p c t i", i=4),
            )
            nc.vector.quantize_mx(
                out=out_codes[:, cols_j].bitcast(FP8X4),
                scales=out_scales[:, cols_j],
                in_=y_woven[:].rearrange("p j t -> p (j t)"),
            )
            nc.sync.dma_start(out_words[:, cols_j], out_codes[:, cols_j].bitcast(I32))
        for q in range(PACK):
            queue = nc.sync if q % 2 == 0 else nc.scalar
            queue.dma_start(
                out_2[0][PACK * q : PACK * (q + 1), :].bitcast(I32),
                out_scales[32 * q : 32 * q + PACK, :].bitcast(I32),
            )
